import numpy as np
import ml_dtypes


def mxq(x, axis, fmt="e4m3"):
    dtype, down = {"e4m3": (ml_dtypes.float8_e4m3fn, 7), "e5m2": (ml_dtypes.float8_e5m2, 14)}[fmt]
    v = np.moveaxis(np.asarray(x, np.float32).astype(ml_dtypes.bfloat16).astype(np.float64), axis, -1)
    blocks = v.reshape(v.shape[:-1] + (-1, 32))
    amax = np.abs(blocks).max(-1, keepdims=True)
    byte = np.maximum(np.where(amax > 0, np.frexp(amax)[1] - 1 + 127, 0) - down, 1)
    scale = np.exp2(byte - 127.0)
    codes = (blocks / scale).astype(np.float32).astype(dtype).astype(np.float64)
    return np.moveaxis((codes * scale).reshape(v.shape), -1, axis)


WIDE = False


def mx_kscale(k):
    if not WIDE:
        return np.ones(k)
    levels = np.array([10, -10, 5, -5, 0])
    if k % 512:
        return np.exp2(np.random.permutation(np.resize(levels, k // 32))).repeat(32)
    a = np.empty((k // 512, 16))
    for p in range(k // 512):
        a[p, :8] = np.random.permutation(np.resize(levels, 8))
        for g in range(8):
            far = levels[np.abs(levels - a[p, g]) >= 10]
            a[p, g + 8] = far[np.random.randint(len(far))]
    return np.exp2(a.ravel()).repeat(32)


def f64(x):
    return np.asarray(x).astype(np.float64)


def striped(idx):
    return np.tile(idx.reshape(-1, 16).T, (8, 1)).astype(np.uint16)


def unstriped(offs):
    return offs[:16].T.reshape(-1).astype(np.int64)


E2M1 = np.array([0.0, 0.5, 1.0, 1.5, 2.0, 3.0, 4.0, 6.0, -0.0, -0.5, -1.0, -1.5, -2.0, -3.0, -4.0, -6.0])


def pack_weight(w, fmt):
    k, n = w.shape
    w = f64(np.asarray(w, np.float32).astype(ml_dtypes.bfloat16)).reshape(k // 32, 32, n)
    amax = np.abs(w).max(1)
    if fmt == "e4m3":
        byte = np.frexp(amax)[1] - 1 + 127 - 7
    else:
        mant, ex = np.frexp(amax / 6.0)
        byte = np.where(mant > 0.5, ex, ex - 1) + 127
    byte = np.clip(np.where(amax > 0, byte, 1), 1, 254)
    scaled = (w * np.exp2(127.0 - byte)[:, None, :]).reshape(k, n).astype(np.float32)
    by_word = np.ascontiguousarray(scaled.reshape(k // 512, 128, 4, n).transpose(0, 1, 3, 2))
    if fmt == "e4m3":
        words = by_word.astype(ml_dtypes.float8_e4m3fn).view(np.uint8)
    else:
        c = by_word.astype(ml_dtypes.float4_e2m1fn).view(np.uint8) & 0xF
        words = (c[..., 0::2] | (c[..., 1::2] << 4)).reshape(k // 512, 128, 2 * n)
    return np.ascontiguousarray(words), np.ascontiguousarray(byte.astype(np.uint8).reshape(k // 512, 16, n))


def unpack_weight(words, scales, fmt):
    g, _, n = scales.shape
    words = np.ascontiguousarray(words).reshape(g, 128, n, -1)
    if fmt == "e4m3":
        vals = words.view(ml_dtypes.float8_e4m3fn).astype(np.float64)
    else:
        nib = np.empty((g, 128, n, 4), np.uint8)
        nib[..., 0::2] = words & 0xF
        nib[..., 1::2] = words >> 4
        vals = E2M1[nib]
    vals = vals * np.repeat(np.exp2(scales.astype(np.float64) - 127.0), 8, axis=1)[..., None]
    return vals.transpose(0, 1, 3, 2).reshape(g * 512, n)


def planes(y):
    n, m = y.shape
    v = y.astype(np.float32).astype(ml_dtypes.bfloat16).astype(np.float64).reshape(n // 32, 32, m)
    top = np.abs(v).max(1)
    byte = np.clip(np.where(top > 0, np.frexp(top)[1] - 1 + 127 - 7, 1), 1, 254)
    codes = (v * np.exp2(127.0 - byte)[:, None, :]).reshape(n, m).astype(np.float32).astype(ml_dtypes.float8_e4m3fn).view(np.uint8)
    words = codes.reshape(n // 512, 128, 4, m).transpose(0, 1, 3, 2)
    return np.ascontiguousarray(words), np.ascontiguousarray(byte.astype(np.uint8).reshape(n // 512, 16, m))


def relu(v):
    return np.maximum(v, 0.0)


K, T, E1, C1, E2, C2, H = 1024, 512, 2, 256, 2, 256, 512
N = 512


def deal(E, C):
    slot_token = np.random.permutation(T)
    return slot_token, None, np.random.uniform(0.2, 1.0, T)


def by_expert(wq, xq, E, C):
    return np.concatenate([wq[e].T @ xq[:, e * C:(e + 1) * C] for e in range(E)], axis=1)


def setup_inputs():
    n = np.random.standard_normal
    s = mx_kscale(K)
    u = mx_kscale(H)
    slots1, pos1, g1 = deal(E1, C1)
    slots2, pos2, g2 = deal(E2, C2)
    x = pack_weight(n((K, T)) * s[:, None], "e4m3")
    w1 = [pack_weight(m, "e2m1") for m in n((E1, K, H)) / np.sqrt(K) / s[None, :, None] * u]
    return {
        "x_words": x[0],
        "x_scales": x[1],
        "w1_words": np.stack([m[0] for m in w1]),
        "w1_scales": np.stack([m[1] for m in w1]),
        "w2": (n((E2, H, N)) / np.sqrt(H) / u[None, :, None]).astype(np.float32),
        "gate1": (np.tile(g1, (128, 1))).astype(np.float32),
        "gate2": (np.tile(g2, (128, 1))).astype(np.float32),
        "offs": striped(slots1),
        "offs2": striped(slots2),
    }


def reference(x_words, x_scales, w1_words, w1_scales, w2, gate1, gate2, offs, offs2):
    w1 = np.stack([unpack_weight(w1_words[e], w1_scales[e], "e2m1") for e in range(E1)])
    w2q = mxq(f64(w2), 1, "e4m3")
    idx, idx2 = unstriped(offs), unstriped(offs2)
    xq = unpack_weight(x_words, x_scales, "e4m3")[:, idx]
    h = relu(by_expert(w1, xq, E1, C1))
    c = np.zeros((H, T))
    c[:, idx] = f64(gate1[:1]) * h
    y = by_expert(w2q, mxq(c[:, idx2], 0, "e4m3"), E2, C2)
    out = np.zeros((N, T))
    out[:, idx2] = f64(gate2[:1]) * y
    out_0 = out
    return (out_0,) + planes(out_0)

@@ -1,0 +1,197 @@
+from contextlib import ExitStack
+
+import concourse.mybir as mybir
+from concourse.masks import make_identity
+
+F32 = mybir.dt.float32
+BF16 = mybir.dt.bfloat16
+I32 = mybir.dt.int32
+U32 = mybir.dt.uint32
+U16 = mybir.dt.uint16
+U8 = mybir.dt.uint8
+FP8X4 = mybir.dt.float8_e4m3fn_x4
+FP4X4 = mybir.dt.float4_e2m1fn_x4
+ACT = mybir.ActivationFunctionType
+MULT = mybir.AluOpType.mult
+
+P = 128
+T = 512
+K = 1024
+H = 512
+N = 512
+EXPERTS = 2
+SLOTS = 256
+PASSES = 2
+PACK = 4
+BLOCKS = T // P
+STRIPE = 16
+HALF = T // 2
+
+FLOPS = 2 * T * (K * H + H * N)
+
+
+def tile_moe_ser_relu_kernel(
+    tc, x_words, x_scales, w1_words, w1_scales, w2, gate1, gate2, offs, offs2, out_0, out_1, out_2
+):
+    nc = tc.nc
+    with ExitStack() as ctx:
+        keep = ctx.enter_context(tc.tile_pool(name="keep", bufs=1))
+        psum = ctx.enter_context(tc.psum_pool(name="psum", bufs=1))
+
+        def sbuf(shape, dtype, name, tag=None):
+            return keep.tile(shape, dtype, name=name, tag=tag or name, align_bytes=64)
+
+        def entries(list_tile, first, count):
+            return list_tile[:, first // STRIPE : (first + count) // STRIPE]
+
+        xs = sbuf([P, PASSES * T], U8, "xs")
+        w1s = sbuf([P, EXPERTS * PASSES * H], U8, "w1s")
+        nc.gpsimd.memset(xs[:].bitcast(I32), 0)
+        nc.gpsimd.memset(w1s[:].bitcast(I32), 0)
+
+        list1 = keep.tile([P, T // STRIPE], U16, name="list1")
+        nc.sync.dma_start(list1[:], offs)
+        xw = [sbuf([P, T], I32, "xw%d" % s) for s in range(PASSES)]
+        for s in range(PASSES):
+            nc.sync.dma_start(xw[s][:], x_words[s].rearrange("p t d -> p (t d)").bitcast(I32))
+        xs_rows = x_scales.bitcast(I32).rearrange("s (q r) w -> r q s w", r=4)
+        for r in range(4):
+            nc.scalar.dma_start(
+                xs[:].bitcast(I32)[r:P:32, :].rearrange("q (s w) -> q s w", s=PASSES), xs_rows[r]
+            )
+        w1w = [sbuf([P, PASSES, 2 * H], U8, "w1w%d" % e) for e in range(EXPERTS)]
+        nc.sync.dma_start(w1w[0][:].bitcast(I32), w1_words[0].bitcast(I32).rearrange("s p w -> p s w"))
+        w1s_rows = w1_scales.bitcast(I32).rearrange("e s (q r) w -> r q (e s) w", r=4)
+        for r in range(4):
+            nc.scalar.dma_start(
+                w1s[:].bitcast(I32)[r:P:32, :].rearrange("q (g w) -> q g w", g=EXPERTS * PASSES), w1s_rows[r]
+            )
+        g1_rows = sbuf([P, P], F32, "g1_rows", tag="late0")
+        nc.sync.dma_start(g1_rows[:], gate1.rearrange("a (b m) -> (a b) m", b=BLOCKS)[0:P, :])
+        nc.sync.dma_start(w1w[1][:].bitcast(I32), w1_words[1].bitcast(I32).rearrange("s p w -> p s w"))
+        list2 = keep.tile([P, T // STRIPE], U16, name="list2")
+        nc.sync.dma_start(list2[:], offs2)
+
+        ident = sbuf([P, P], F32, "ident")
+        make_identity(nc, ident[:])
+        g1_t = psum.tile([P, P], F32, name="g1_t", tag="turn3")
+        nc.tensor.transpose(g1_t[:], g1_rows[:], ident[:])
+        g1_col = sbuf([P, BLOCKS], F32, "g1_col")
+        nc.scalar.activation(g1_col[:], g1_t[:, 0:BLOCKS], ACT.Copy)
+
+        w2_raw = [None, None]
+        w2_raw[0] = sbuf([P, PACK, N], F32, "w2_raw0", tag="late0")
+        nc.sync.dma_start(w2_raw[0][:], w2[0].rearrange("(p j) n -> p j n", j=PACK))
+
+        gw = [sbuf([P, T], U32, "gw%d" % s) for s in range(PASSES)]
+        gs = [sbuf([P, T], U8, "gs%d" % s) for s in range(PASSES)]
+        for first, count in ((0, P), (P, P), (2 * P, 2 * P)):
+            cols = slice(first, first + count)
+            for s in range(PASSES):
+                nc.vector.tensor_copy(gw[s][:, cols], xw[s][:].bitcast(U32).indirect(entries(list1, first, count)))
+            for s in range(PASSES):
+                nc.vector.tensor_copy(gs[s][:, cols], xs[:, s * T : (s + 1) * T].indirect(entries(list1, first, count)))
+
+        c_slots = sbuf([P, 2, T], F32, "c_slots")
+        c_tok = [sbuf([P, T], F32, "c_tok%d" % u) for u in range(2)]
+        for b in range(BLOCKS):
+            e = b * P // SLOTS
+            cols = slice(b * P, (b + 1) * P)
+            h_ps = psum.tile([P, H], F32, name="h_ps%d" % b, tag="sum%d" % b)
+            for s in range(PASSES):
+                g = e * PASSES + s
+                nc.tensor.matmul_mx(
+                    out=h_ps[:],
+                    lhsT=gw[s][:, cols].bitcast(FP8X4),
+                    lhsT_scale=gs[s][:, cols],
+                    rhs=w1w[e][:, s, :].bitcast(FP4X4),
+                    rhs_scale=w1s[:, g * H : (g + 1) * H],
+                    start=(s == 0),
+                    stop=(s == PASSES - 1),
+                )
+            h = sbuf([P, H], F32, "h%d" % b)
+            nc.scalar.activation(h[:], h_ps[:], ACT.Relu)
+            c_rows = sbuf([P, H], BF16, "c_rows%d" % b)
+            nc.scalar.activation(
+                c_rows[:].rearrange("m (u p d) -> m u p d", u=2, d=2),
+                h[:].rearrange("m (p u d) -> m u p d", u=2, d=2),
+                ACT.Copy,
+                scale=g1_col[:, b : b + 1],
+            )
+            c_ps = psum.tile([P, 2, P], F32, name="c_ps%d" % b, tag="turn%d" % b)
+            for u in range(2):
+                nc.tensor.transpose(c_ps[:, u, :], c_rows[:].bitcast(F32)[:, u * P : (u + 1) * P], ident[:])
+            nc.scalar.copy(c_slots[:, :, cols], c_ps[:])
+            for u in range(2):
+                nc.vector.tensor_copy(c_tok[u][:].indirect(entries(list1, b * P, P)), c_slots[:, u, cols])
+
+        w2_raw[1] = sbuf([P, PACK, N], F32, "w2_raw1", tag="h0")
+        nc.sync.dma_start(w2_raw[1][:], w2[1].rearrange("(p j) n -> p j n", j=PACK))
+        g2 = sbuf([P, T], F32, "g2", tag="h1")
+        nc.sync.dma_start(g2[:], gate2)
+
+        w2_bf = [sbuf([P, PACK * N], BF16, "w2_bf0", tag="c_rows3"), sbuf([P, PACK * N], BF16, "w2_bf1", tag="c_rows2")]
+        for f in range(EXPERTS):
+            nc.scalar.copy(
+                w2_bf[f][:].rearrange("p (t m j) -> p m j t", t=PACK, j=PACK),
+                w2_raw[f][:].rearrange("p j (m t) -> p m j t", t=PACK),
+            )
+        cq = sbuf([P, T], U32, "cq")
+        cq_s = sbuf([P, T], U8, "cq_s")
+        y = sbuf([P, PACK, T], F32, "y")
+        for f in range(EXPERTS):
+            cols = slice(f * SLOTS, (f + 1) * SLOTS)
+            c_in = sbuf([P, SLOTS, 2], U32, "c_in%d" % f)
+            for u in range(2):
+                nc.vector.tensor_copy(c_in[:, :, u], c_tok[u][:].bitcast(U32).indirect(entries(list2, f * SLOTS, SLOTS)))
+            w2q = sbuf([P, N], U32, "w2q%d" % f)
+            w2q_s = sbuf([P, N], U8, "w2q_s%d" % f)
+            nc.vector.quantize_mx(out=w2q[:].bitcast(FP8X4), scales=w2q_s[:], in_=w2_bf[f][:])
+            nc.vector.quantize_mx(
+                out=cq[:, cols].bitcast(FP8X4),
+                scales=cq_s[:, cols],
+                in_=c_in[:].rearrange("p m u -> p (m u)").bitcast(BF16),
+            )
+            for pair in range(2):
+                y_ps = psum.tile([P, 2, SLOTS], F32, name="y_ps%d%d" % (f, pair), tag="sum%d" % (2 * f + pair))
+                for i in range(2):
+                    t = 2 * pair + i
+                    nc.tensor.matmul_mx(
+                        out=y_ps[:, i, :],
+                        lhsT=w2q[:, t * P : (t + 1) * P].bitcast(FP8X4),
+                        lhsT_scale=w2q_s[:, t * P : (t + 1) * P],
+                        rhs=cq[:, cols].bitcast(FP8X4),
+                        rhs_scale=cq_s[:, cols],
+                        start=True,
+                        stop=True,
+                    )
+                nc.scalar.copy(y[:, 2 * pair : 2 * pair + 2, cols], y_ps[:])
+
+        o_tok = [sbuf([P, T], F32, "o_tok%d" % t) for t in range(PACK)]
+        o_bf = [sbuf([P, HALF, PACK], BF16, "o_bf%d" % a) for a in range(2)]
+        out_rows = out_0.rearrange("(p t) c -> t p c", t=PACK)
+        for f in range(EXPERTS):
+            cols = slice(f * SLOTS, (f + 1) * SLOTS)
+            for t in range(PACK):
+                nc.vector.tensor_tensor(
+                    o_tok[t][:].indirect(entries(list2, f * SLOTS, SLOTS)), y[:, t, cols], g2[:, cols], MULT
+                )
+                if f == EXPERTS - 1:
+                    nc.sync.dma_start(out_rows[t], o_tok[t][:])
+                    nc.scalar.copy(o_bf[0][:, :, t], o_tok[t][:, 0:HALF])
+                    if t < 2:
+                        nc.scalar.copy(o_bf[1][:, :, t], o_tok[t][:, HALF:T])
+        for t in (2, 3):
+            nc.vector.tensor_copy(o_bf[1][:, :, t], o_tok[t][:, HALF:T])
+
+        oq_s = sbuf([P, T], U8, "oq_s")
+        words_out = out_1[0].rearrange("p t d -> p (t d)").bitcast(I32)
+        for a in (1, 0):
+            cols = slice(a * HALF, (a + 1) * HALF)
+            oq = sbuf([P, HALF], U32, "oq%d" % a)
+            nc.vector.quantize_mx(
+                out=oq[:].bitcast(FP8X4), scales=oq_s[:, cols], in_=o_bf[a][:].rearrange("p c t -> p (c t)")
+            )
+            nc.sync.dma_start(words_out[:, cols], oq[:].bitcast(I32))
+        for q in range(4):
+            nc.scalar.dma_start(out_2[0].bitcast(I32)[4 * q : 4 * q + 4, :], oq_s[:].bitcast(I32)[32 * q : 32 * q + 4, :])

@@ -27,6 +27,8 @@ BLOCKS = T // P
 STRIPE = 16
 HALF = T // 2
 
+PLANE_ORDER = ((0, 1, 2, 3), (2, 0, 1, 3))
+
 FLOPS = 2 * T * (K * H + H * N)
 
 
@@ -46,58 +48,54 @@ def tile_moe_ser_relu_kernel(
 
         xs = sbuf([P, PASSES * T], U8, "xs")
         w1s = sbuf([P, EXPERTS * PASSES * H], U8, "w1s")
-        nc.gpsimd.memset(xs[:].bitcast(I32), 0)
-        nc.gpsimd.memset(w1s[:].bitcast(I32), 0)
+        nc.vector.memset(xs[:].bitcast(I32), 0)
+        nc.vector.memset(w1s[:].bitcast(I32), 0)
 
         list1 = keep.tile([P, T // STRIPE], U16, name="list1")
-        nc.sync.dma_start(list1[:], offs)
         xw = [sbuf([P, T], I32, "xw%d" % s) for s in range(PASSES)]
         for s in range(PASSES):
             nc.sync.dma_start(xw[s][:], x_words[s].rearrange("p t d -> p (t d)").bitcast(I32))
         xs_rows = x_scales.bitcast(I32).rearrange("s (q r) w -> r q s w", r=4)
         for r in range(4):
-            nc.scalar.dma_start(
+            nc.sync.dma_start(
                 xs[:].bitcast(I32)[r:P:32, :].rearrange("q (s w) -> q s w", s=PASSES), xs_rows[r]
             )
+        nc.sync.dma_start(list1[:], offs)
         w1w = [sbuf([P, PASSES, 2 * H], U8, "w1w%d" % e) for e in range(EXPERTS)]
         nc.sync.dma_start(w1w[0][:].bitcast(I32), w1_words[0].bitcast(I32).rearrange("s p w -> p s w"))
-        w1s_rows = w1_scales.bitcast(I32).rearrange("e s (q r) w -> r q (e s) w", r=4)
-        for r in range(4):
-            nc.scalar.dma_start(
-                w1s[:].bitcast(I32)[r:P:32, :].rearrange("q (g w) -> q g w", g=EXPERTS * PASSES), w1s_rows[r]
-            )
         g1_rows = sbuf([P, P], F32, "g1_rows", tag="late0")
         nc.sync.dma_start(g1_rows[:], gate1.rearrange("a (b m) -> (a b) m", b=BLOCKS)[0:P, :])
+        w1s_rows = w1_scales.bitcast(I32).rearrange("e s (q r) w -> r q (e s) w", r=4)
+        for r in range(4):
+            nc.sync.dma_start(
+                w1s[:].bitcast(I32)[r:P:32, :].rearrange("q (g w) -> q g w", g=EXPERTS * PASSES), w1s_rows[r]
+            )
         nc.sync.dma_start(w1w[1][:].bitcast(I32), w1_words[1].bitcast(I32).rearrange("s p w -> p s w"))
         list2 = keep.tile([P, T // STRIPE], U16, name="list2")
         nc.sync.dma_start(list2[:], offs2)
 
         ident = sbuf([P, P], F32, "ident")
         make_identity(nc, ident[:])
-        g1_t = psum.tile([P, P], F32, name="g1_t", tag="turn3")
-        nc.tensor.transpose(g1_t[:], g1_rows[:], ident[:])
-        g1_col = sbuf([P, BLOCKS], F32, "g1_col")
-        nc.scalar.activation(g1_col[:], g1_t[:, 0:BLOCKS], ACT.Copy)
-
-        w2_raw = [None, None]
-        w2_raw[0] = sbuf([P, PACK, N], F32, "w2_raw0", tag="late0")
-        nc.sync.dma_start(w2_raw[0][:], w2[0].rearrange("(p j) n -> p j n", j=PACK))
 
         gw = [sbuf([P, T], U32, "gw%d" % s) for s in range(PASSES)]
         gs = [sbuf([P, T], U8, "gs%d" % s) for s in range(PASSES)]
-        for first, count in ((0, P), (P, P), (2 * P, 2 * P)):
+        for first, count in ((0, P), (P, P), (2 * P, P), (3 * P, P)):
             cols = slice(first, first + count)
             for s in range(PASSES):
                 nc.vector.tensor_copy(gw[s][:, cols], xw[s][:].bitcast(U32).indirect(entries(list1, first, count)))
             for s in range(PASSES):
                 nc.vector.tensor_copy(gs[s][:, cols], xs[:, s * T : (s + 1) * T].indirect(entries(list1, first, count)))
 
+        g1_col = sbuf([P, BLOCKS], F32, "g1_col")
+        g1_t = psum.tile([P, P], F32, name="g1_t", tag="bank5")
+        nc.tensor.transpose(g1_t[:], g1_rows[:], ident[:])
+        nc.scalar.activation(g1_col[:], g1_t[:, 0:BLOCKS], ACT.Copy)
         c_slots = sbuf([P, 2, T], F32, "c_slots")
         c_tok = [sbuf([P, T], F32, "c_tok%d" % u) for u in range(2)]
         for b in range(BLOCKS):
             e = b * P // SLOTS
             cols = slice(b * P, (b + 1) * P)
-            h_ps = psum.tile([P, H], F32, name="h_ps%d" % b, tag="sum%d" % b)
+            h_ps = psum.tile([P, H], F32, name="h_ps%d" % b, tag=("bank0", "bank1", "bank0", "bank2")[b])
             for s in range(PASSES):
                 g = e * PASSES + s
                 nc.tensor.matmul_mx(
@@ -109,28 +107,30 @@ def tile_moe_ser_relu_kernel(
                     start=(s == 0),
                     stop=(s == PASSES - 1),
                 )
-            h = sbuf([P, H], F32, "h%d" % b)
-            nc.scalar.activation(h[:], h_ps[:], ACT.Relu)
-            c_rows = sbuf([P, H], BF16, "c_rows%d" % b)
-            nc.scalar.activation(
-                c_rows[:].rearrange("m (u p d) -> m u p d", u=2, d=2),
-                h[:].rearrange("m (p u d) -> m u p d", u=2, d=2),
-                ACT.Copy,
-                scale=g1_col[:, b : b + 1],
-            )
-            c_ps = psum.tile([P, 2, P], F32, name="c_ps%d" % b, tag="turn%d" % b)
-            for u in range(2):
-                nc.tensor.transpose(c_ps[:, u, :], c_rows[:].bitcast(F32)[:, u * P : (u + 1) * P], ident[:])
-            nc.scalar.copy(c_slots[:, :, cols], c_ps[:])
-            for u in range(2):
-                nc.vector.tensor_copy(c_tok[u][:].indirect(entries(list1, b * P, P)), c_slots[:, u, cols])
+            h = sbuf([P, 2, P, 2], F32, "h%d" % b)
+            c_rows = sbuf([P, 2, P, 2], BF16, "c_rows%d" % b)
+            c_words = c_rows[:].rearrange("m u p d -> m u (p d)").bitcast(F32)
+            for us in ([slice(0, 1), slice(1, 2)] if b == 0 else [slice(0, 2)]):
+                nc.scalar.activation(
+                    h[:, us], h_ps[:].rearrange("m (p u d) -> m u p d", u=2, d=2)[:, us], ACT.Relu
+                )
+                nc.scalar.activation(c_rows[:, us], h[:, us], ACT.Copy, scale=g1_col[:, b : b + 1])
+                c_ps = psum.tile([P, 2, P], F32, name="c_ps%d%d" % (b, us.start), tag=("bank2", "bank4", "bank5", "bank1")[b] if us.start == 0 else "bank3")
+                for u in range(us.start, us.stop):
+                    nc.tensor.transpose(c_ps[:, u, :], c_words[:, u, 0:P] , ident[:])
+                nc.scalar.copy(c_slots[:, us, cols], c_ps[:, us, :])
+                for u in range(us.start, us.stop):
+                    nc.vector.tensor_copy(c_tok[u][:].indirect(entries(list1, b * P, P)), c_slots[:, u, cols])
 
+        w2_raw = [None, None]
+        w2_raw[0] = sbuf([P, PACK, N], F32, "w2_raw0", tag="late0")
+        nc.sync.dma_start(w2_raw[0][:], w2[0].rearrange("(p j) n -> p j n", j=PACK))
         w2_raw[1] = sbuf([P, PACK, N], F32, "w2_raw1", tag="h0")
         nc.sync.dma_start(w2_raw[1][:], w2[1].rearrange("(p j) n -> p j n", j=PACK))
         g2 = sbuf([P, T], F32, "g2", tag="h1")
         nc.sync.dma_start(g2[:], gate2)
 
-        w2_bf = [sbuf([P, PACK * N], BF16, "w2_bf0", tag="c_rows3"), sbuf([P, PACK * N], BF16, "w2_bf1", tag="c_rows2")]
+        w2_bf = [sbuf([P, PACK * N], BF16, "w2_bf0", tag="c_rows3"), sbuf([P, PACK * N], BF16, "w2_bf1", tag="c_slots")]
         for f in range(EXPERTS):
             nc.scalar.copy(
                 w2_bf[f][:].rearrange("p (t m j) -> p m j t", t=PACK, j=PACK),
@@ -138,10 +138,10 @@ def tile_moe_ser_relu_kernel(
             )
         cq = sbuf([P, T], U32, "cq")
         cq_s = sbuf([P, T], U8, "cq_s")
-        y = sbuf([P, PACK, T], F32, "y")
+        y = {}
         for f in range(EXPERTS):
             cols = slice(f * SLOTS, (f + 1) * SLOTS)
-            c_in = sbuf([P, SLOTS, 2], U32, "c_in%d" % f)
+            c_in = sbuf([P, SLOTS, 2], U32, "c_in%d" % f, tag=("c_in0", "c_rows3")[f])
             for u in range(2):
                 nc.vector.tensor_copy(c_in[:, :, u], c_tok[u][:].bitcast(U32).indirect(entries(list2, f * SLOTS, SLOTS)))
             w2q = sbuf([P, N], U32, "w2q%d" % f)
@@ -152,10 +152,11 @@ def tile_moe_ser_relu_kernel(
                 scales=cq_s[:, cols],
                 in_=c_in[:].rearrange("p m u -> p (m u)").bitcast(BF16),
             )
+            order = PLANE_ORDER[f]
             for pair in range(2):
-                y_ps = psum.tile([P, 2, SLOTS], F32, name="y_ps%d%d" % (f, pair), tag="sum%d" % (2 * f + pair))
+                y_ps = psum.tile([P, 2, SLOTS], F32, name="y_ps%d%d" % (f, pair), tag=("bank6", "bank7", "bank3", "bank4")[2 * f + pair])
                 for i in range(2):
-                    t = 2 * pair + i
+                    t = order[2 * pair + i]
                     nc.tensor.matmul_mx(
                         out=y_ps[:, i, :],
                         lhsT=w2q[:, t * P : (t + 1) * P].bitcast(FP8X4),
@@ -165,24 +166,32 @@ def tile_moe_ser_relu_kernel(
                         start=True,
                         stop=True,
                     )
-                nc.scalar.copy(y[:, 2 * pair : 2 * pair + 2, cols], y_ps[:])
+                for i in range(2):
+                    t = order[2 * pair + i]
+                    if (f, t) == (1, 3):
+                        last_ps = y_ps
+                    else:
+                        y[f, t] = sbuf([P, SLOTS], F32, "y%d%d" % (f, t))
+                        nc.scalar.copy(y[f, t][:], y_ps[:, i, :])
 
         o_tok = [sbuf([P, T], F32, "o_tok%d" % t) for t in range(PACK)]
         o_bf = [sbuf([P, HALF, PACK], BF16, "o_bf%d" % a) for a in range(2)]
         out_rows = out_0.rearrange("(p t) c -> t p c", t=PACK)
         for f in range(EXPERTS):
             cols = slice(f * SLOTS, (f + 1) * SLOTS)
-            for t in range(PACK):
+            for t in PLANE_ORDER[f]:
                 nc.vector.tensor_tensor(
-                    o_tok[t][:].indirect(entries(list2, f * SLOTS, SLOTS)), y[:, t, cols], g2[:, cols], MULT
+                    o_tok[t][:].indirect(entries(list2, f * SLOTS, SLOTS)), y[f, t][:], g2[:, cols], MULT
                 )
                 if f == EXPERTS - 1:
                     nc.sync.dma_start(out_rows[t], o_tok[t][:])
                     nc.scalar.copy(o_bf[0][:, :, t], o_tok[t][:, 0:HALF])
-                    if t < 2:
+                    if t < 3:
                         nc.scalar.copy(o_bf[1][:, :, t], o_tok[t][:, HALF:T])
-        for t in (2, 3):
-            nc.vector.tensor_copy(o_bf[1][:, :, t], o_tok[t][:, HALF:T])
+                    if t == 2:
+                        y[1, 3] = sbuf([P, SLOTS], F32, "y13", tag="y12")
+                        nc.scalar.copy(y[1, 3][:], last_ps[:, 1, :])
+        nc.vector.tensor_copy(o_bf[1][:, :, 3], o_tok[3][:, HALF:T])
 
         oq_s = sbuf([P, T], U8, "oq_s")
         words_out = out_1[0].rearrange("p t d -> p (t d)").bitcast(I32)

@@ -13,6 +13,7 @@ FP8X4 = mybir.dt.float8_e4m3fn_x4
 FP4X4 = mybir.dt.float4_e2m1fn_x4
 ACT = mybir.ActivationFunctionType
 MULT = mybir.AluOpType.mult
+MAX = mybir.AluOpType.max
 
 P = 128
 T = 512
@@ -27,7 +28,7 @@ BLOCKS = T // P
 STRIPE = 16
 HALF = T // 2
 
-PLANE_ORDER = ((0, 1, 2, 3), (2, 0, 1, 3))
+PLANE_ORDER = (2, 0, 1, 3)
 
 FLOPS = 2 * T * (K * H + H * N)
 
@@ -38,6 +39,7 @@ def tile_moe_ser_relu_kernel(
     nc = tc.nc
     with ExitStack() as ctx:
         keep = ctx.enter_context(tc.tile_pool(name="keep", bufs=1))
+        shared = ctx.enter_context(tc.tile_pool(name="shared", bufs=1))
         psum = ctx.enter_context(tc.psum_pool(name="psum", bufs=1))
 
         def sbuf(shape, dtype, name, tag=None):
@@ -77,125 +79,164 @@ def tile_moe_ser_relu_kernel(
         ident = sbuf([P, P], F32, "ident")
         make_identity(nc, ident[:])
 
-        gw = [sbuf([P, T], U32, "gw%d" % s) for s in range(PASSES)]
-        gs = [sbuf([P, T], U8, "gs%d" % s) for s in range(PASSES)]
-        for first, count in ((0, P), (P, P), (2 * P, P), (3 * P, P)):
-            cols = slice(first, first + count)
-            for s in range(PASSES):
-                nc.vector.tensor_copy(gw[s][:, cols], xw[s][:].bitcast(U32).indirect(entries(list1, first, count)))
-            for s in range(PASSES):
-                nc.vector.tensor_copy(gs[s][:, cols], xs[:, s * T : (s + 1) * T].indirect(entries(list1, first, count)))
-
-        g1_col = sbuf([P, BLOCKS], F32, "g1_col")
-        g1_t = psum.tile([P, P], F32, name="g1_t", tag="bank5")
+        g1_t = psum.tile([P, P], F32, name="g1_t", tag="bank7")
         nc.tensor.transpose(g1_t[:], g1_rows[:], ident[:])
+        g1_first = shared.tile([P, 32], F32, name="g1_first", offset=192, align_bytes=64)
+        nc.scalar.activation(g1_first[:, 0:1], g1_t[:, 0:1], ACT.Copy)
+        g1_col = sbuf([P, BLOCKS], F32, "g1_col")
         nc.scalar.activation(g1_col[:], g1_t[:, 0:BLOCKS], ACT.Copy)
+
+        gw, gs = {}, {}
+
+        def gather_words(b, tile):
+            for s in range(PASSES):
+                gw[b, s] = tile[:, s, :]
+                nc.vector.tensor_copy(gw[b, s], xw[s][:].bitcast(U32).indirect(entries(list1, b * P, P)))
+
+        def gather_scales(b, blocks, s, tile):
+            nc.vector.tensor_copy(tile[:], xs[:, s * T : (s + 1) * T].indirect(entries(list1, b * P, blocks * P)))
+            for i in range(blocks):
+                gs[b + i, s] = tile[:, i * P : (i + 1) * P]
+
+        for b in range(2):
+            gather_words(b, sbuf([P, PASSES, P], U32, "gw%d" % b))
+            for s in range(PASSES):
+                gather_scales(b, 1, s, sbuf([P, P], U8, "gs%d%d" % (b, s)))
+        gather_words(2, sbuf([P, PASSES, P], U32, "gw2"))
+        gather_scales(2, 2, 0, sbuf([P, SLOTS], U8, "gs20"))
+
         c_slots = sbuf([P, 2, T], F32, "c_slots")
         c_tok = [sbuf([P, T], F32, "c_tok%d" % u) for u in range(2)]
         for b in range(BLOCKS):
             e = b * P // SLOTS
             cols = slice(b * P, (b + 1) * P)
-            h_ps = psum.tile([P, H], F32, name="h_ps%d" % b, tag=("bank0", "bank1", "bank0", "bank2")[b])
+            h_ps = psum.tile([P, H], F32, name="h_ps%d" % b, tag="bank%d" % b)
             for s in range(PASSES):
                 g = e * PASSES + s
                 nc.tensor.matmul_mx(
                     out=h_ps[:],
-                    lhsT=gw[s][:, cols].bitcast(FP8X4),
-                    lhsT_scale=gs[s][:, cols],
+                    lhsT=gw[b, s].bitcast(FP8X4),
+                    lhsT_scale=gs[b, s],
                     rhs=w1w[e][:, s, :].bitcast(FP4X4),
                     rhs_scale=w1s[:, g * H : (g + 1) * H],
                     start=(s == 0),
                     stop=(s == PASSES - 1),
                 )
-            h = sbuf([P, 2, P, 2], F32, "h%d" % b)
             c_rows = sbuf([P, 2, P, 2], BF16, "c_rows%d" % b)
+            h_sorted = h_ps[:].rearrange("m (p u d) -> m u p d", u=2, d=2)
+            if b == 0:
+                nc.vector.tensor_scalar(c_rows[:], h_sorted, 0.0, g1_first[:, 0:1], MAX, MULT)
+                gather_scales(2, 2, 1, shared.tile([P, SLOTS], U8, name="gs21", offset=0, align_bytes=64))
+                gather_words(3, shared.tile([P, PASSES, P], U32, name="gw3", offset=256, align_bytes=64))
+            else:
+                h = sbuf([P, 2, P, 2], F32, "h%d" % b)
+                nc.scalar.activation(h[:], h_sorted, ACT.Relu)
+                nc.scalar.activation(c_rows[:], h[:], ACT.Copy, scale=g1_col[:, b : b + 1])
             c_words = c_rows[:].rearrange("m u p d -> m u (p d)").bitcast(F32)
-            for us in ([slice(0, 1), slice(1, 2)] if b == 0 else [slice(0, 2)]):
-                nc.scalar.activation(
-                    h[:, us], h_ps[:].rearrange("m (p u d) -> m u p d", u=2, d=2)[:, us], ACT.Relu
-                )
-                nc.scalar.activation(c_rows[:, us], h[:, us], ACT.Copy, scale=g1_col[:, b : b + 1])
-                c_ps = psum.tile([P, 2, P], F32, name="c_ps%d%d" % (b, us.start), tag=("bank2", "bank4", "bank5", "bank1")[b] if us.start == 0 else "bank3")
-                for u in range(us.start, us.stop):
-                    nc.tensor.transpose(c_ps[:, u, :], c_words[:, u, 0:P] , ident[:])
-                nc.scalar.copy(c_slots[:, us, cols], c_ps[:, us, :])
-                for u in range(us.start, us.stop):
-                    nc.vector.tensor_copy(c_tok[u][:].indirect(entries(list1, b * P, P)), c_slots[:, u, cols])
+            c_ps = psum.tile([P, 2, P], F32, name="c_ps%d" % b, tag="bank%d" % (4 + b))
+            for u in range(2):
+                nc.tensor.transpose(c_ps[:, u, :], c_words[:, u, :], ident[:])
+            nc.scalar.copy(c_slots[:, :, cols], c_ps[:])
+            for u in range(2):
+                nc.vector.tensor_copy(c_tok[u][:].indirect(entries(list1, b * P, P)), c_slots[:, u, cols])
 
-        w2_raw = [None, None]
-        w2_raw[0] = sbuf([P, PACK, N], F32, "w2_raw0", tag="late0")
-        nc.sync.dma_start(w2_raw[0][:], w2[0].rearrange("(p j) n -> p j n", j=PACK))
-        w2_raw[1] = sbuf([P, PACK, N], F32, "w2_raw1", tag="h0")
-        nc.sync.dma_start(w2_raw[1][:], w2[1].rearrange("(p j) n -> p j n", j=PACK))
-        g2 = sbuf([P, T], F32, "g2", tag="h1")
+        w2_raw = [sbuf([P, PACK, N], F32, "w2_raw0", tag="late0"), sbuf([P, PACK, N], F32, "w2_raw1", tag="h1")]
+        for f in range(EXPERTS):
+            nc.sync.dma_start(w2_raw[f][:], w2[f].rearrange("(p j) n -> p j n", j=PACK))
+        g2 = sbuf([P, T], F32, "g2", tag="h2")
         nc.sync.dma_start(g2[:], gate2)
 
-        w2_bf = [sbuf([P, PACK * N], BF16, "w2_bf0", tag="c_rows3"), sbuf([P, PACK * N], BF16, "w2_bf1", tag="c_slots")]
-        for f in range(EXPERTS):
-            nc.scalar.copy(
-                w2_bf[f][:].rearrange("p (t m j) -> p m j t", t=PACK, j=PACK),
-                w2_raw[f][:].rearrange("p j (m t) -> p m j t", t=PACK),
-            )
         cq = sbuf([P, T], U32, "cq")
         cq_s = sbuf([P, T], U8, "cq_s")
-        y = {}
-        for f in range(EXPERTS):
-            cols = slice(f * SLOTS, (f + 1) * SLOTS)
-            c_in = sbuf([P, SLOTS, 2], U32, "c_in%d" % f, tag=("c_in0", "c_rows3")[f])
+        w2q, w2q_s, y, y_ps, c_pairs = {}, {}, {}, {}, {}
+
+        def quantise_w2(f, tag):
+            w2_bf = sbuf([P, PACK * N], BF16, "w2_bf%d" % f, tag=tag)
+            nc.scalar.copy(
+                w2_bf[:].rearrange("p (t m j) -> p m j t", t=PACK, j=PACK),
+                w2_raw[f][:].rearrange("p j (m t) -> p m j t", t=PACK),
+            )
+            w2q[f] = sbuf([P, N], U32, "w2q%d" % f)
+            w2q_s[f] = sbuf([P, N], U8, "w2q_s%d" % f)
+            nc.vector.quantize_mx(out=w2q[f][:].bitcast(FP8X4), scales=w2q_s[f][:], in_=w2_bf[:])
+
+        def gather_c(f, tag):
+            c_pairs[f] = sbuf([P, 2, SLOTS], U32, "c_pairs%d" % f, tag=tag)
             for u in range(2):
-                nc.vector.tensor_copy(c_in[:, :, u], c_tok[u][:].bitcast(U32).indirect(entries(list2, f * SLOTS, SLOTS)))
-            w2q = sbuf([P, N], U32, "w2q%d" % f)
-            w2q_s = sbuf([P, N], U8, "w2q_s%d" % f)
-            nc.vector.quantize_mx(out=w2q[:].bitcast(FP8X4), scales=w2q_s[:], in_=w2_bf[f][:])
+                nc.vector.tensor_copy(
+                    c_pairs[f][:, u, :], c_tok[u][:].bitcast(U32).indirect(entries(list2, f * SLOTS, SLOTS))
+                )
+
+        def quantise_c(f, tag):
+            cols = slice(f * SLOTS, (f + 1) * SLOTS)
+            c_in = sbuf([P, SLOTS, 2], U32, "c_in%d" % f, tag=tag)
+            nc.scalar.copy(c_in[:], c_pairs[f][:].rearrange("p u m -> p m u"))
             nc.vector.quantize_mx(
                 out=cq[:, cols].bitcast(FP8X4),
                 scales=cq_s[:, cols],
                 in_=c_in[:].rearrange("p m u -> p (m u)").bitcast(BF16),
             )
-            order = PLANE_ORDER[f]
-            for pair in range(2):
-                y_ps = psum.tile([P, 2, SLOTS], F32, name="y_ps%d%d" % (f, pair), tag=("bank6", "bank7", "bank3", "bank4")[2 * f + pair])
-                for i in range(2):
-                    t = order[2 * pair + i]
-                    nc.tensor.matmul_mx(
-                        out=y_ps[:, i, :],
-                        lhsT=w2q[:, t * P : (t + 1) * P].bitcast(FP8X4),
-                        lhsT_scale=w2q_s[:, t * P : (t + 1) * P],
-                        rhs=cq[:, cols].bitcast(FP8X4),
-                        rhs_scale=cq_s[:, cols],
-                        start=True,
-                        stop=True,
-                    )
-                for i in range(2):
-                    t = order[2 * pair + i]
-                    if (f, t) == (1, 3):
-                        last_ps = y_ps
-                    else:
-                        y[f, t] = sbuf([P, SLOTS], F32, "y%d%d" % (f, t))
-                        nc.scalar.copy(y[f, t][:], y_ps[:, i, :])
+
+        def multiply(f):
+            cols = slice(f * SLOTS, (f + 1) * SLOTS)
+            for i, t in enumerate(PLANE_ORDER):
+                y_ps[f, t] = psum.tile([P, SLOTS], F32, name="y_ps%d%d" % (f, t), tag="bank%d" % (PACK * f + i))
+                nc.tensor.matmul_mx(
+                    out=y_ps[f, t][:],
+                    lhsT=w2q[f][:, t * P : (t + 1) * P].bitcast(FP8X4),
+                    lhsT_scale=w2q_s[f][:, t * P : (t + 1) * P],
+                    rhs=cq[:, cols].bitcast(FP8X4),
+                    rhs_scale=cq_s[:, cols],
+                    start=True,
+                    stop=True,
+                )
+
+        def evacuate(f, t, tag=None):
+            y[f, t] = sbuf([P, SLOTS], F32, "y%d%d" % (f, t), tag=tag)
+            nc.scalar.copy(y[f, t][:], y_ps[f, t][:])
 
         o_tok = [sbuf([P, T], F32, "o_tok%d" % t) for t in range(PACK)]
+
+        def scatter(f, t):
+            nc.vector.tensor_tensor(
+                o_tok[t][:].indirect(entries(list2, f * SLOTS, SLOTS)),
+                y[f, t][:],
+                g2[:, f * SLOTS : (f + 1) * SLOTS],
+                MULT,
+            )
+
+        quantise_w2(0, "c_rows3")
+        gather_c(0, None)
+        quantise_c(0, None)
+        gather_c(1, "c_in0")
+        multiply(0)
+        for t in PLANE_ORDER[:2]:
+            evacuate(0, t)
+            scatter(0, t)
+        quantise_c(1, "w2q0")
+        quantise_w2(1, "c_in0")
+        evacuate(0, PLANE_ORDER[2], "h1")
+        scatter(0, PLANE_ORDER[2])
+        evacuate(0, PLANE_ORDER[3])
+        scatter(0, PLANE_ORDER[3])
+        multiply(1)
+        for t in PLANE_ORDER[:3]:
+            evacuate(1, t)
+
         o_bf = [sbuf([P, HALF, PACK], BF16, "o_bf%d" % a) for a in range(2)]
         out_rows = out_0.rearrange("(p t) c -> t p c", t=PACK)
-        for f in range(EXPERTS):
-            cols = slice(f * SLOTS, (f + 1) * SLOTS)
-            for t in PLANE_ORDER[f]:
-                nc.vector.tensor_tensor(
-                    o_tok[t][:].indirect(entries(list2, f * SLOTS, SLOTS)), y[f, t][:], g2[:, cols], MULT
-                )
-                if f == EXPERTS - 1:
-                    nc.sync.dma_start(out_rows[t], o_tok[t][:])
-                    nc.scalar.copy(o_bf[0][:, :, t], o_tok[t][:, 0:HALF])
-                    if t < 3:
-                        nc.scalar.copy(o_bf[1][:, :, t], o_tok[t][:, HALF:T])
-                    if t == 2:
-                        y[1, 3] = sbuf([P, SLOTS], F32, "y13", tag="y12")
-                        nc.scalar.copy(y[1, 3][:], last_ps[:, 1, :])
-        nc.vector.tensor_copy(o_bf[1][:, :, 3], o_tok[3][:, HALF:T])
+        for t in PLANE_ORDER:
+            scatter(1, t)
+            nc.sync.dma_start(out_rows[t], o_tok[t][:])
+            cast = nc.vector.tensor_copy if t == 3 else nc.scalar.copy
+            for a in range(2):
+                cast(o_bf[a][:, :, t], o_tok[t][:, a * HALF : (a + 1) * HALF])
+            if t == 2:
+                evacuate(1, 3, "y12")
 
         oq_s = sbuf([P, T], U8, "oq_s")
         words_out = out_1[0].rearrange("p t d -> p (t d)").bitcast(I32)
-        for a in (1, 0):
+        for a in range(2):
             cols = slice(a * HALF, (a + 1) * HALF)
             oq = sbuf([P, HALF], U32, "oq%d" % a)
             nc.vector.quantize_mx(
@@ -203,4 +244,5 @@ def tile_moe_ser_relu_kernel(
             )
             nc.sync.dma_start(words_out[:, cols], oq[:].bitcast(I32))
         for q in range(4):
-            nc.scalar.dma_start(out_2[0].bitcast(I32)[4 * q : 4 * q + 4, :], oq_s[:].bitcast(I32)[32 * q : 32 * q + 4, :])
+            queue = nc.scalar if q < 2 else nc.sync
+            queue.dma_start(out_2[0].bitcast(I32)[4 * q : 4 * q + 4, :], oq_s[:].bitcast(I32)[32 * q : 32 * q + 4, :])

@@ -63,7 +63,7 @@ def tile_moe_ser_relu_kernel(
                 xs[:].bitcast(I32)[r:P:32, :].rearrange("q (s w) -> q s w", s=PASSES), xs_rows[r]
             )
         nc.sync.dma_start(list1[:], offs)
-        w1w = [sbuf([P, PASSES, 2 * H], U8, "w1w%d" % e) for e in range(EXPERTS)]
+        w1w = [sbuf([P, PASSES, 2 * H], U8, "w1w0")]
         nc.sync.dma_start(w1w[0][:].bitcast(I32), w1_words[0].bitcast(I32).rearrange("s p w -> p s w"))
         g1_rows = sbuf([P, P], F32, "g1_rows", tag="late0")
         nc.sync.dma_start(g1_rows[:], gate1.rearrange("a (b m) -> (a b) m", b=BLOCKS)[0:P, :])
@@ -72,7 +72,6 @@ def tile_moe_ser_relu_kernel(
             nc.sync.dma_start(
                 w1s[:].bitcast(I32)[r:P:32, :].rearrange("q (g w) -> q g w", g=EXPERTS * PASSES), w1s_rows[r]
             )
-        nc.sync.dma_start(w1w[1][:].bitcast(I32), w1_words[1].bitcast(I32).rearrange("s p w -> p s w"))
         list2 = keep.tile([P, T // STRIPE], U16, name="list2")
         nc.sync.dma_start(list2[:], offs2)
 
@@ -85,6 +84,9 @@ def tile_moe_ser_relu_kernel(
         nc.scalar.activation(g1_first[:, 0:1], g1_t[:, 0:1], ACT.Copy)
         g1_col = sbuf([P, BLOCKS], F32, "g1_col")
         nc.scalar.activation(g1_col[:], g1_t[:, 0:BLOCKS], ACT.Copy)
+
+        w1w.append(sbuf([P, PASSES, 2 * H], U8, "w1w1", tag="late0"))
+        nc.sync.dma_start(w1w[1][:].bitcast(I32), w1_words[1].bitcast(I32).rearrange("s p w -> p s w"))
 
         gw, gs = {}, {}
 
@@ -140,7 +142,7 @@ def tile_moe_ser_relu_kernel(
             for u in range(2):
                 nc.vector.tensor_copy(c_tok[u][:].indirect(entries(list1, b * P, P)), c_slots[:, u, cols])
 
-        w2_raw = [sbuf([P, PACK, N], F32, "w2_raw0", tag="late0"), sbuf([P, PACK, N], F32, "w2_raw1", tag="h1")]
+        w2_raw = [sbuf([P, PACK, N], F32, "w2_raw0", tag="gw0"), sbuf([P, PACK, N], F32, "w2_raw1", tag="h1")]
         for f in range(EXPERTS):
             nc.sync.dma_start(w2_raw[f][:], w2[f].rearrange("(p j) n -> p j n", j=PACK))
         g2 = sbuf([P, T], F32, "g2", tag="h2")
@@ -228,15 +230,19 @@ def tile_moe_ser_relu_kernel(
         for t in PLANE_ORDER:
             scatter(1, t)
             nc.sync.dma_start(out_rows[t], o_tok[t][:])
-            cast = nc.vector.tensor_copy if t == 3 else nc.scalar.copy
-            for a in range(2):
-                cast(o_bf[a][:, :, t], o_tok[t][:, a * HALF : (a + 1) * HALF])
+            if t < 3:
+                for a in (1, 0):
+                    nc.scalar.copy(o_bf[a][:, :, t], o_tok[t][:, a * HALF : (a + 1) * HALF])
+            else:
+                nc.vector.tensor_copy(o_bf[1][:, :, t], o_tok[t][:, HALF:T])
+                nc.vector.tensor_copy(o_bf[0][:, P:HALF, t], o_tok[t][:, P:HALF])
+                nc.scalar.copy(o_bf[0][:, 0:P, t], o_tok[t][:, 0:P])
             if t == 2:
                 evacuate(1, 3, "y12")
 
         oq_s = sbuf([P, T], U8, "oq_s")
         words_out = out_1[0].rearrange("p t d -> p (t d)").bitcast(I32)
-        for a in range(2):
+        for a in (1, 0):
             cols = slice(a * HALF, (a + 1) * HALF)
             oq = sbuf([P, HALF], U32, "oq%d" % a)
             nc.vector.quantize_mx(

from contextlib import ExitStack

import concourse.mybir as mybir
from concourse.masks import make_identity

F32 = mybir.dt.float32
BF16 = mybir.dt.bfloat16
I32 = mybir.dt.int32
U32 = mybir.dt.uint32
U16 = mybir.dt.uint16
U8 = mybir.dt.uint8
FP8X4 = mybir.dt.float8_e4m3fn_x4
FP4X4 = mybir.dt.float4_e2m1fn_x4
ACT = mybir.ActivationFunctionType
MULT = mybir.AluOpType.mult
MAX = mybir.AluOpType.max

P = 128
T = 512
K = 1024
H = 512
N = 512
EXPERTS = 2
SLOTS = 256
PASSES = 2
PACK = 4
BLOCKS = T // P
STRIPE = 16
HALF = T // 2

PLANE_ORDER = (2, 0, 1, 3)

FLOPS = 2 * T * (K * H + H * N)


def tile_moe_ser_relu_kernel(
    tc, x_words, x_scales, w1_words, w1_scales, w2, gate1, gate2, offs, offs2, out_0, out_1, out_2
):
    nc = tc.nc
    with ExitStack() as ctx:
        keep = ctx.enter_context(tc.tile_pool(name="keep", bufs=1))
        shared = ctx.enter_context(tc.tile_pool(name="shared", bufs=1))
        psum = ctx.enter_context(tc.psum_pool(name="psum", bufs=1))

        def sbuf(shape, dtype, name, tag=None):
            return keep.tile(shape, dtype, name=name, tag=tag or name, align_bytes=64)

        def entries(list_tile, first, count):
            return list_tile[:, first // STRIPE : (first + count) // STRIPE]

        xs = sbuf([P, PASSES * T], U8, "xs")
        w1s = sbuf([P, EXPERTS * PASSES * H], U8, "w1s")
        nc.vector.memset(xs[:].bitcast(I32), 0)
        nc.vector.memset(w1s[:].bitcast(I32), 0)

        list1 = keep.tile([P, T // STRIPE], U16, name="list1")
        xw = [sbuf([P, T], I32, "xw%d" % s) for s in range(PASSES)]
        for s in range(PASSES):
            nc.sync.dma_start(xw[s][:], x_words[s].rearrange("p t d -> p (t d)").bitcast(I32))
        xs_rows = x_scales.bitcast(I32).rearrange("s (q r) w -> r q s w", r=4)
        for r in range(4):
            nc.sync.dma_start(
                xs[:].bitcast(I32)[r:P:32, :].rearrange("q (s w) -> q s w", s=PASSES), xs_rows[r]
            )
        nc.sync.dma_start(list1[:], offs)
        w1w = [sbuf([P, PASSES, 2 * H], U8, "w1w0")]
        nc.sync.dma_start(w1w[0][:].bitcast(I32), w1_words[0].bitcast(I32).rearrange("s p w -> p s w"))
        g1_rows = sbuf([P, P], F32, "g1_rows", tag="late0")
        nc.sync.dma_start(g1_rows[:], gate1.rearrange("a (b m) -> (a b) m", b=BLOCKS)[0:P, :])
        w1s_rows = w1_scales.bitcast(I32).rearrange("e s (q r) w -> r q (e s) w", r=4)
        for r in range(4):
            nc.sync.dma_start(
                w1s[:].bitcast(I32)[r:P:32, :].rearrange("q (g w) -> q g w", g=EXPERTS * PASSES), w1s_rows[r]
            )
        list2 = keep.tile([P, T // STRIPE], U16, name="list2")
        nc.sync.dma_start(list2[:], offs2)

        ident = sbuf([P, P], F32, "ident")
        make_identity(nc, ident[:])

        g1_t = psum.tile([P, P], F32, name="g1_t", tag="bank7")
        nc.tensor.transpose(g1_t[:], g1_rows[:], ident[:])
        g1_first = shared.tile([P, 32], F32, name="g1_first", offset=192, align_bytes=64)
        nc.scalar.activation(g1_first[:, 0:1], g1_t[:, 0:1], ACT.Copy)
        g1_col = sbuf([P, BLOCKS], F32, "g1_col")
        nc.scalar.activation(g1_col[:], g1_t[:, 0:BLOCKS], ACT.Copy)

        w1w.append(sbuf([P, PASSES, 2 * H], U8, "w1w1", tag="late0"))
        nc.sync.dma_start(w1w[1][:].bitcast(I32), w1_words[1].bitcast(I32).rearrange("s p w -> p s w"))

        gw, gs = {}, {}

        def gather_words(b, tile):
            for s in range(PASSES):
                gw[b, s] = tile[:, s, :]
                nc.vector.tensor_copy(gw[b, s], xw[s][:].bitcast(U32).indirect(entries(list1, b * P, P)))

        def gather_scales(b, blocks, s, tile):
            nc.vector.tensor_copy(tile[:], xs[:, s * T : (s + 1) * T].indirect(entries(list1, b * P, blocks * P)))
            for i in range(blocks):
                gs[b + i, s] = tile[:, i * P : (i + 1) * P]

        for b in range(2):
            gather_words(b, sbuf([P, PASSES, P], U32, "gw%d" % b))
            for s in range(PASSES):
                gather_scales(b, 1, s, sbuf([P, P], U8, "gs%d%d" % (b, s)))
        gather_words(2, sbuf([P, PASSES, P], U32, "gw2"))
        gather_scales(2, 2, 0, sbuf([P, SLOTS], U8, "gs20"))

        c_slots = sbuf([P, 2, T], F32, "c_slots")
        c_tok = [sbuf([P, T], F32, "c_tok%d" % u) for u in range(2)]
        for b in range(BLOCKS):
            e = b * P // SLOTS
            cols = slice(b * P, (b + 1) * P)
            h_ps = psum.tile([P, H], F32, name="h_ps%d" % b, tag="bank%d" % b)
            for s in range(PASSES):
                g = e * PASSES + s
                nc.tensor.matmul_mx(
                    out=h_ps[:],
                    lhsT=gw[b, s].bitcast(FP8X4),
                    lhsT_scale=gs[b, s],
                    rhs=w1w[e][:, s, :].bitcast(FP4X4),
                    rhs_scale=w1s[:, g * H : (g + 1) * H],
                    start=(s == 0),
                    stop=(s == PASSES - 1),
                )
            c_rows = sbuf([P, 2, P, 2], BF16, "c_rows%d" % b)
            h_sorted = h_ps[:].rearrange("m (p u d) -> m u p d", u=2, d=2)
            if b == 0:
                nc.vector.tensor_scalar(c_rows[:], h_sorted, 0.0, g1_first[:, 0:1], MAX, MULT)
                gather_scales(2, 2, 1, shared.tile([P, SLOTS], U8, name="gs21", offset=0, align_bytes=64))
                gather_words(3, shared.tile([P, PASSES, P], U32, name="gw3", offset=256, align_bytes=64))
            else:
                h = sbuf([P, 2, P, 2], F32, "h%d" % b)
                nc.scalar.activation(h[:], h_sorted, ACT.Relu)
                nc.scalar.activation(c_rows[:], h[:], ACT.Copy, scale=g1_col[:, b : b + 1])
            c_words = c_rows[:].rearrange("m u p d -> m u (p d)").bitcast(F32)
            c_ps = psum.tile([P, 2, P], F32, name="c_ps%d" % b, tag="bank%d" % (4 + b))
            for u in range(2):
                nc.tensor.transpose(c_ps[:, u, :], c_words[:, u, :], ident[:])
            nc.scalar.copy(c_slots[:, :, cols], c_ps[:])
            for u in range(2):
                nc.vector.tensor_copy(c_tok[u][:].indirect(entries(list1, b * P, P)), c_slots[:, u, cols])

        w2_raw = [sbuf([P, PACK, N], F32, "w2_raw0", tag="gw0"), sbuf([P, PACK, N], F32, "w2_raw1", tag="h1")]
        for f in range(EXPERTS):
            nc.sync.dma_start(w2_raw[f][:], w2[f].rearrange("(p j) n -> p j n", j=PACK))
        g2 = sbuf([P, T], F32, "g2", tag="h2")
        nc.sync.dma_start(g2[:], gate2)

        cq = sbuf([P, T], U32, "cq")
        cq_s = sbuf([P, T], U8, "cq_s")
        w2q, w2q_s, y, y_ps, c_pairs = {}, {}, {}, {}, {}

        def quantise_w2(f, tag):
            w2_bf = sbuf([P, PACK * N], BF16, "w2_bf%d" % f, tag=tag)
            nc.scalar.copy(
                w2_bf[:].rearrange("p (t m j) -> p m j t", t=PACK, j=PACK),
                w2_raw[f][:].rearrange("p j (m t) -> p m j t", t=PACK),
            )
            w2q[f] = sbuf([P, N], U32, "w2q%d" % f)
            w2q_s[f] = sbuf([P, N], U8, "w2q_s%d" % f)
            nc.vector.quantize_mx(out=w2q[f][:].bitcast(FP8X4), scales=w2q_s[f][:], in_=w2_bf[:])

        def gather_c(f, tag):
            c_pairs[f] = sbuf([P, 2, SLOTS], U32, "c_pairs%d" % f, tag=tag)
            for u in range(2):
                nc.vector.tensor_copy(
                    c_pairs[f][:, u, :], c_tok[u][:].bitcast(U32).indirect(entries(list2, f * SLOTS, SLOTS))
                )

        def quantise_c(f, tag):
            cols = slice(f * SLOTS, (f + 1) * SLOTS)
            c_in = sbuf([P, SLOTS, 2], U32, "c_in%d" % f, tag=tag)
            nc.scalar.copy(c_in[:], c_pairs[f][:].rearrange("p u m -> p m u"))
            nc.vector.quantize_mx(
                out=cq[:, cols].bitcast(FP8X4),
                scales=cq_s[:, cols],
                in_=c_in[:].rearrange("p m u -> p (m u)").bitcast(BF16),
            )

        def multiply(f):
            cols = slice(f * SLOTS, (f + 1) * SLOTS)
            for i, t in enumerate(PLANE_ORDER):
                y_ps[f, t] = psum.tile([P, SLOTS], F32, name="y_ps%d%d" % (f, t), tag="bank%d" % (PACK * f + i))
                nc.tensor.matmul_mx(
                    out=y_ps[f, t][:],
                    lhsT=w2q[f][:, t * P : (t + 1) * P].bitcast(FP8X4),
                    lhsT_scale=w2q_s[f][:, t * P : (t + 1) * P],
                    rhs=cq[:, cols].bitcast(FP8X4),
                    rhs_scale=cq_s[:, cols],
                    start=True,
                    stop=True,
                )

        def evacuate(f, t, tag=None):
            y[f, t] = sbuf([P, SLOTS], F32, "y%d%d" % (f, t), tag=tag)
            nc.scalar.copy(y[f, t][:], y_ps[f, t][:])

        o_tok = [sbuf([P, T], F32, "o_tok%d" % t) for t in range(PACK)]

        def scatter(f, t):
            nc.vector.tensor_tensor(
                o_tok[t][:].indirect(entries(list2, f * SLOTS, SLOTS)),
                y[f, t][:],
                g2[:, f * SLOTS : (f + 1) * SLOTS],
                MULT,
            )

        quantise_w2(0, "c_rows3")
        gather_c(0, None)
        quantise_c(0, None)
        gather_c(1, "c_in0")
        multiply(0)
        for t in PLANE_ORDER[:2]:
            evacuate(0, t)
            scatter(0, t)
        quantise_c(1, "w2q0")
        quantise_w2(1, "c_in0")
        evacuate(0, PLANE_ORDER[2], "h1")
        scatter(0, PLANE_ORDER[2])
        evacuate(0, PLANE_ORDER[3])
        scatter(0, PLANE_ORDER[3])
        multiply(1)
        for t in PLANE_ORDER[:3]:
            evacuate(1, t)

        o_bf = [sbuf([P, HALF, PACK], BF16, "o_bf%d" % a) for a in range(2)]
        out_rows = out_0.rearrange("(p t) c -> t p c", t=PACK)
        for t in PLANE_ORDER:
            scatter(1, t)
            nc.sync.dma_start(out_rows[t], o_tok[t][:])
            if t < 3:
                for a in (1, 0):
                    nc.scalar.copy(o_bf[a][:, :, t], o_tok[t][:, a * HALF : (a + 1) * HALF])
            else:
                nc.vector.tensor_copy(o_bf[1][:, :, t], o_tok[t][:, HALF:T])
                nc.vector.tensor_copy(o_bf[0][:, P:HALF, t], o_tok[t][:, P:HALF])
                nc.scalar.copy(o_bf[0][:, 0:P, t], o_tok[t][:, 0:P])
            if t == 2:
                evacuate(1, 3, "y12")

        oq_s = sbuf([P, T], U8, "oq_s")
        words_out = out_1[0].rearrange("p t d -> p (t d)").bitcast(I32)
        for a in (1, 0):
            cols = slice(a * HALF, (a + 1) * HALF)
            oq = sbuf([P, HALF], U32, "oq%d" % a)
            nc.vector.quantize_mx(
                out=oq[:].bitcast(FP8X4), scales=oq_s[:, cols], in_=o_bf[a][:].rearrange("p c t -> p (c t)")
            )
            nc.sync.dma_start(words_out[:, cols], oq[:].bitcast(I32))
        for q in range(4):
            queue = nc.scalar if q < 2 else nc.sync
            queue.dma_start(out_2[0].bitcast(I32)[4 * q : 4 * q + 4, :], oq_s[:].bitcast(I32)[32 * q : 32 * q + 4, :])
